import numpy as np
import ml_dtypes


def mxq(x, axis, fmt="e4m3"):
    dtype, down = {"e4m3": (ml_dtypes.float8_e4m3fn, 7), "e5m2": (ml_dtypes.float8_e5m2, 14)}[fmt]
    v = np.moveaxis(np.asarray(x, np.float32).astype(ml_dtypes.bfloat16).astype(np.float64), axis, -1)
    blocks = v.reshape(v.shape[:-1] + (-1, 32))
    amax = np.abs(blocks).max(-1, keepdims=True)
    byte = np.maximum(np.where(amax > 0, np.frexp(amax)[1] - 1 + 127, 0) - down, 1)
    scale = np.exp2(byte - 127.0)
    codes = (blocks / scale).astype(np.float32).astype(dtype).astype(np.float64)
    return np.moveaxis((codes * scale).reshape(v.shape), -1, axis)


WIDE = False


def mx_kscale(k):
    if not WIDE:
        return np.ones(k)
    levels = np.array([10, -10, 5, -5, 0])
    if k % 512:
        return np.exp2(np.random.permutation(np.resize(levels, k // 32))).repeat(32)
    a = np.empty((k // 512, 16))
    for p in range(k // 512):
        a[p, :8] = np.random.permutation(np.resize(levels, 8))
        for g in range(8):
            far = levels[np.abs(levels - a[p, g]) >= 10]
            a[p, g + 8] = far[np.random.randint(len(far))]
    return np.exp2(a.ravel()).repeat(32)


def f64(x):
    return np.asarray(x).astype(np.float64)


def striped(idx):
    return np.tile(idx.reshape(-1, 16).T, (8, 1)).astype(np.uint16)


def unstriped(offs):
    return offs[:16].T.reshape(-1).astype(np.int64)


def silu(v):
    return v / (1.0 + np.exp(-np.maximum(v, -700.0)))


K, T, E, C, H, N = 512, 512, 4, 256, 512, 256


def by_expert(wq, xq):
    return np.concatenate([wq[e].T @ xq[:, e * C:(e + 1) * C] for e in range(E)], axis=1)


def setup_inputs():
    n = np.random.standard_normal
    s = mx_kscale(K)[:, None]
    u = mx_kscale(H)
    first = np.random.permutation(np.repeat(np.arange(E), T // E))
    second = (first + 1 + np.random.permutation(np.repeat(np.arange(E - 1), -(-T // (E - 1)))[:T])) % E
    while np.bincount(second, minlength=E).max() != T // E:
        load = np.bincount(second, minlength=E); hi, lo = int(load.argmax()), int(load.argmin())
        t = np.flatnonzero((second == hi) & (first != lo))[0]; second[t] = lo
    slot_token = np.empty(E * C, np.int64); pos = np.empty((2, T), np.int64); fill = np.zeros(E, np.int64)
    place = np.stack([np.random.permutation(C) for _ in range(E)])
    for r, deal in enumerate((first, second)):
        for t in np.random.permutation(T):
            e = deal[t]; j = e * C + place[e, fill[e]]; fill[e] += 1; slot_token[j] = t; pos[r, t] = j
    g = np.random.uniform(0.2, 0.8, T)
    return {
        "xT": (n((K, T)) * s).astype(np.float32),
        "w1": (n((E, K, H)) / np.sqrt(K) / s[None] * u[None, None, :]).astype(np.float32),
        "w2": (n((E, H, N)) / np.sqrt(H) / u[None, :, None]).astype(np.float32),
        "gate": np.stack([np.tile(g, (N, 1)), np.tile(1.0 - g, (N, 1))]).astype(np.float32),
        "offs": striped(slot_token),
        "pos1": striped(pos[0]),
        "pos2": striped(pos[1]),
    }


def reference(xT, w1, w2, gate, offs, pos1, pos2):
    idx = unstriped(offs)
    xq = mxq(f64(xT)[:, idx], 0, "e4m3")
    h = silu(by_expert(mxq(f64(w1), 1, "e4m3"), xq))
    y = by_expert(mxq(f64(w2), 1, "e4m3"), mxq(h, 0, "e4m3"))
    return f64(gate[0]) * y[:, unstriped(pos1)] + f64(gate[1]) * y[:, unstriped(pos2)]

@@ -1,0 +1,206 @@
+from contextlib import ExitStack
+
+import concourse.mybir as mybir
+
+K, T, E, C, H, N = 512, 512, 4, 256, 512, 256
+FLOPS = 2 * E * C * (K * H + H * N)
+
+P = 128
+PACK = 4
+HALF = T // 2
+SLOTS = 128
+BLOCKS = N // P
+W1_VECTOR = (40, 64, 88, 104)
+W2_VECTOR = (False, False, False, True)
+
+F32 = mybir.dt.float32
+BF16 = mybir.dt.bfloat16
+U32 = mybir.dt.uint32
+U16 = mybir.dt.uint16
+U8 = mybir.dt.uint8
+FP8X4 = mybir.dt.float8_e4m3fn_x4
+MULT = mybir.AluOpType.mult
+SILU = mybir.ActivationFunctionType.Silu
+
+
+def tile_routed_moe_kernel(tc, xT, w1, w2, gate, offs, pos1, pos2, out):
+    nc = tc.nc
+    with ExitStack() as ctx:
+        lists = ctx.enter_context(tc.tile_pool(name="lists", bufs=1))
+        keep = ctx.enter_context(tc.tile_pool(name="keep", bufs=1))
+        four = ctx.enter_context(tc.tile_pool(name="four", bufs=4))
+        psum = ctx.enter_context(tc.psum_pool(name="psum", bufs=4))
+
+        offs_sb = lists.tile([P, E * C // 16], U16)
+        pos1_sb = lists.tile([P, T // 16], U16)
+        pos2_sb = lists.tile([P, T // 16], U16)
+
+        dummy = keep.tile([P, 2], F32)
+        nc.gpsimd.memset(dummy[:], 0.0)
+        nc.scalar.activation(dummy[:, 1:2], dummy[:, 0:1], SILU)
+
+        x_view = xT.rearrange("(p j) t -> p j t", j=PACK)
+        x_raw = []
+        for a in range(2):
+            x_half = keep.tile([P, PACK, HALF], F32, name=f"x_raw{a}")
+            nc.sync.dma_start(out=x_half[:], in_=x_view[:, :, a * HALF : (a + 1) * HALF])
+            x_raw.append(x_half)
+            if a == 0:
+                nc.sync.dma_start(out=offs_sb[:], in_=offs)
+        w1_raw = []
+        w2_raw = []
+
+        def load_w1(e):
+            w1_tile = four.tile([P, PACK, H], F32, name="w1_tile")
+            nc.sync.dma_start(out=w1_tile[:], in_=w1[e].rearrange("(p j) h -> p j h", j=PACK))
+            w1_raw.append(w1_tile)
+
+        def load_w2(e):
+            w2_tile = four.tile([P, PACK, N], F32, name="w2_tile")
+            nc.sync.dma_start(out=w2_tile[:], in_=w2[e].rearrange("(p j) n -> p j n", j=PACK))
+            w2_raw.append(w2_tile)
+
+        load_w1(0)
+        load_w1(1)
+        load_w2(0)
+        load_w1(2)
+        load_w2(1)
+        load_w1(3)
+        load_w2(2)
+        nc.sync.dma_start(out=pos1_sb[:], in_=pos1)
+        nc.sync.dma_start(out=pos2_sb[:], in_=pos2)
+        load_w2(3)
+        gates = []
+        for b in range(BLOCKS):
+            gate_tile = keep.tile([P, 2, T], F32, name=f"gate{b}")
+            nc.sync.dma_start(out=gate_tile[:], in_=gate[:, b * P : (b + 1) * P, :].rearrange("g p t -> p g t"))
+            gates.append(gate_tile)
+
+        x_grouped = keep.tile([P, T, PACK], BF16, align_bytes=64)
+        x_codes = keep.tile([P, T], U32, align_bytes=64)
+        x_scales = keep.tile([P, T], U8, align_bytes=64)
+        for a in range(2):
+            for part, copy in ((0, nc.vector.tensor_copy), (1, nc.scalar.copy)):
+                c0 = part * 128
+                dst = x_grouped[:, a * HALF + c0 : a * HALF + c0 + 128, :]
+                src = x_raw[a][:, :, c0 : c0 + 128]
+                copy(out=dst.rearrange("p (c i) j -> p c j i", i=4), in_=src.rearrange("p j (c i) -> p c j i", i=4))
+        for a in range(2):
+            cols = slice(a * HALF, (a + 1) * HALF)
+            nc.vector.quantize_mx(
+                out=x_codes[:, cols].bitcast(FP8X4),
+                scales=x_scales[:, cols],
+                in_=x_grouped[:, cols, :].rearrange("p t j -> p (t j)"),
+            )
+
+        y_slots = []
+        for b in range(BLOCKS):
+            y_block = keep.tile([P, E * C], F32, name=f"y_slots{b}")
+            y_slots.append(y_block)
+
+        w1_q = []
+        w2_q = []
+        g_q = []
+
+        def interleave_w1(e):
+            grouped = four.tile([P, H * PACK], BF16, name="w1_grouped", align_bytes=64)
+            dst = grouped[:].rearrange("p (t m j) -> p m j t", t=PACK, j=PACK)
+            src = w1_raw[e][:].rearrange("p j (m t) -> p m j t", t=PACK)
+            nc.vector.tensor_copy(out=dst[:, :W1_VECTOR[e]], in_=src[:, :W1_VECTOR[e]])
+            nc.scalar.copy(out=dst[:, W1_VECTOR[e]:], in_=src[:, W1_VECTOR[e]:])
+            return grouped
+
+        def quantize_w1(grouped):
+            codes = four.tile([P, H], U32, name="w1_codes", align_bytes=64)
+            scales = four.tile([P, H], U8, name="w1_scales", align_bytes=64)
+            nc.vector.quantize_mx(out=codes[:].bitcast(FP8X4), scales=scales[:], in_=grouped[:])
+            w1_q.append((codes, scales))
+
+        def gather(e):
+            index = offs_sb[:, e * C // 16 : (e + 1) * C // 16]
+            codes = four.tile([P, C], U32, name="slot_codes", align_bytes=64)
+            scales = four.tile([P, C], U8, name="slot_scales", align_bytes=64)
+            nc.vector.tensor_copy(out=codes[:], in_=x_codes[:].indirect(index))
+            nc.vector.tensor_copy(out=scales[:], in_=x_scales[:].indirect(index))
+            g_q.append((codes, scales))
+
+        def interleave_w2(e):
+            grouped = four.tile([P, N, PACK], BF16, name="w2_grouped", align_bytes=64)
+            copy = nc.vector.tensor_copy if W2_VECTOR[e] else nc.scalar.copy
+            copy(
+                out=grouped[:].rearrange("p (c i) j -> p c j i", i=4),
+                in_=w2_raw[e][:].rearrange("p j (c i) -> p c j i", i=4),
+            )
+            return grouped
+
+        def quantize_w2(grouped):
+            codes = four.tile([P, N], U32, name="w2_codes", align_bytes=64)
+            scales = four.tile([P, N], U8, name="w2_scales", align_bytes=64)
+            nc.vector.quantize_mx(
+                out=codes[:].bitcast(FP8X4), scales=scales[:], in_=grouped[:].rearrange("p n j -> p (n j)")
+            )
+            w2_q.append((codes, scales))
+
+        def first_layer(e):
+            grouped = four.tile([P, C, PACK], BF16, name="h_grouped", align_bytes=64)
+            for s in range(C // SLOTS):
+                cols = slice(s * SLOTS, (s + 1) * SLOTS)
+                acc = psum.tile([P, PACK, SLOTS], F32, name="h_acc")
+                for t in range(PACK):
+                    nc.tensor.matmul_mx(
+                        out=acc[:, t, :],
+                        lhsT=w1_q[e][0][:, t * P : (t + 1) * P].bitcast(FP8X4),
+                        lhsT_scale=w1_q[e][1][:, t * P : (t + 1) * P],
+                        rhs=g_q[e][0][:, cols].bitcast(FP8X4),
+                        rhs_scale=g_q[e][1][:, cols],
+                        start=True,
+                        stop=True,
+                    )
+                nc.scalar.activation(grouped[:, cols, :], acc[:].rearrange("p t n -> p n t"), SILU)
+            return grouped
+
+        def second_layer(e, grouped):
+            codes = four.tile([P, C], U32, name="h_codes", align_bytes=64)
+            scales = four.tile([P, C], U8, name="h_scales", align_bytes=64)
+            nc.vector.quantize_mx(
+                out=codes[:].bitcast(FP8X4), scales=scales[:], in_=grouped[:].rearrange("p n t -> p (n t)")
+            )
+            acc = psum.tile([P, BLOCKS, C], F32, name="y_acc")
+            for b in range(BLOCKS):
+                nc.tensor.matmul_mx(
+                    out=acc[:, b, :],
+                    lhsT=w2_q[e][0][:, b * P : (b + 1) * P].bitcast(FP8X4),
+                    lhsT_scale=w2_q[e][1][:, b * P : (b + 1) * P],
+                    rhs=codes[:].bitcast(FP8X4),
+                    rhs_scale=scales[:],
+                    start=True,
+                    stop=True,
+                )
+            for b in range(BLOCKS):
+                nc.scalar.copy(out=y_slots[b][:, e * C : (e + 1) * C], in_=acc[:, b, :])
+
+        h_groups = []
+        for e in range(E + 1):
+            if e < E:
+                gather(e)
+                w1_grouped = interleave_w1(e)
+                quantize_w1(w1_grouped)
+                h_groups.append(first_layer(e))
+            if e > 0:
+                w2_grouped = interleave_w2(e - 1)
+                quantize_w2(w2_grouped)
+                second_layer(e - 1, h_groups[e - 1])
+
+        out_view = out.rearrange("(b p) t -> b p t", p=P)
+        parts = []
+        for b in range(BLOCKS):
+            pair = []
+            for r, index in ((0, pos1_sb), (1, pos2_sb)):
+                part = keep.tile([P, T], F32, name=f"part{b}{r}")
+                nc.vector.tensor_tensor(part[:], y_slots[b][:].indirect(index[:]), gates[b][:, r, :], MULT)
+                pair.append(part)
+            parts.append(pair)
+        for b in range(BLOCKS):
+            total = keep.tile([P, T], F32, name=f"total{b}")
+            nc.vector.tensor_add(out=total[:], in0=parts[b][0][:], in1=parts[b][1][:])
+            nc.sync.dma_start(out=out_view[b], in_=total[:])

@@ -10,8 +10,11 @@ PACK = 4
 HALF = T // 2
 SLOTS = 128
 BLOCKS = N // P
-W1_VECTOR = (40, 64, 88, 104)
-W2_VECTOR = (False, False, False, True)
+X_VECTOR = (192, 128)
+W1_VECTOR = (0, 16, 56, 128)
+W1_GPSIMD = (0, 0, 0, 0)
+W2_ENGINE = "VSVV"
+PIECES = (384, 384, 256)
 
 F32 = mybir.dt.float32
 BF16 = mybir.dt.bfloat16
@@ -20,6 +23,7 @@ U16 = mybir.dt.uint16
 U8 = mybir.dt.uint8
 FP8X4 = mybir.dt.float8_e4m3fn_x4
 MULT = mybir.AluOpType.mult
+ADD = mybir.AluOpType.add
 SILU = mybir.ActivationFunctionType.Silu
 
 
@@ -28,8 +32,8 @@ def tile_routed_moe_kernel(tc, xT, w1, w2, gate, offs, pos1, pos2, out):
     with ExitStack() as ctx:
         lists = ctx.enter_context(tc.tile_pool(name="lists", bufs=1))
         keep = ctx.enter_context(tc.tile_pool(name="keep", bufs=1))
-        four = ctx.enter_context(tc.tile_pool(name="four", bufs=4))
         psum = ctx.enter_context(tc.psum_pool(name="psum", bufs=4))
+        ysum = ctx.enter_context(tc.psum_pool(name="ysum", bufs=1))
 
         offs_sb = lists.tile([P, E * C // 16], U16)
         pos1_sb = lists.tile([P, T // 16], U16)
@@ -39,51 +43,45 @@ def tile_routed_moe_kernel(tc, xT, w1, w2, gate, offs, pos1, pos2, out):
         nc.gpsimd.memset(dummy[:], 0.0)
         nc.scalar.activation(dummy[:, 1:2], dummy[:, 0:1], SILU)
 
+        def gp_copy(out, in_):
+            nc.gpsimd.tensor_scalar(out=out, in0=in_, scalar1=1.0, scalar2=0.0, op0=MULT, op1=ADD)
+
+        copy_on = {"V": nc.vector.tensor_copy, "S": nc.scalar.copy, "G": gp_copy}
+
         x_view = xT.rearrange("(p j) t -> p j t", j=PACK)
-        x_raw = []
-        for a in range(2):
-            x_half = keep.tile([P, PACK, HALF], F32, name=f"x_raw{a}")
-            nc.sync.dma_start(out=x_half[:], in_=x_view[:, :, a * HALF : (a + 1) * HALF])
-            x_raw.append(x_half)
-            if a == 0:
+        x_raw = {}
+        w1_raw = {}
+        w2_raw = {}
+        gates = {}
+
+        def load(what, i):
+            if what == "x":
+                x_raw[i] = keep.tile([P, PACK, HALF], F32, name=f"x_raw{i}")
+                nc.sync.dma_start(out=x_raw[i][:], in_=x_view[:, :, i * HALF : (i + 1) * HALF])
+            elif what == "w1":
+                w1_raw[i] = keep.tile([P, PACK, H], F32, name=f"w1_raw{i}")
+                nc.sync.dma_start(out=w1_raw[i][:], in_=w1[i].rearrange("(p j) h -> p j h", j=PACK))
+            elif what == "w2":
+                w2_raw[i] = keep.tile([P, PACK, N], F32, name=f"w2_raw{i}")
+                nc.sync.dma_start(out=w2_raw[i][:], in_=w2[i].rearrange("(p j) n -> p j n", j=PACK))
+            elif what == "g":
+                gates[i] = keep.tile([P, 2, T], F32, name=f"gate{i}")
+                nc.sync.dma_start(out=gates[i][:], in_=gate[:, i * P : (i + 1) * P, :].rearrange("g p t -> p g t"))
+            elif what == "o":
                 nc.sync.dma_start(out=offs_sb[:], in_=offs)
-        w1_raw = []
-        w2_raw = []
+            elif what == "p":
+                nc.sync.dma_start(out=(pos1_sb if i == 0 else pos2_sb)[:], in_=(pos1 if i == 0 else pos2))
 
-        def load_w1(e):
-            w1_tile = four.tile([P, PACK, H], F32, name="w1_tile")
-            nc.sync.dma_start(out=w1_tile[:], in_=w1[e].rearrange("(p j) h -> p j h", j=PACK))
-            w1_raw.append(w1_tile)
-
-        def load_w2(e):
-            w2_tile = four.tile([P, PACK, N], F32, name="w2_tile")
-            nc.sync.dma_start(out=w2_tile[:], in_=w2[e].rearrange("(p j) n -> p j n", j=PACK))
-            w2_raw.append(w2_tile)
-
-        load_w1(0)
-        load_w1(1)
-        load_w2(0)
-        load_w1(2)
-        load_w2(1)
-        load_w1(3)
-        load_w2(2)
-        nc.sync.dma_start(out=pos1_sb[:], in_=pos1)
-        nc.sync.dma_start(out=pos2_sb[:], in_=pos2)
-        load_w2(3)
-        gates = []
-        for b in range(BLOCKS):
-            gate_tile = keep.tile([P, 2, T], F32, name=f"gate{b}")
-            nc.sync.dma_start(out=gate_tile[:], in_=gate[:, b * P : (b + 1) * P, :].rearrange("g p t -> p g t"))
-            gates.append(gate_tile)
+        for what, i in (("x", 0), ("o", 0), ("x", 1), ("w1", 0), ("w1", 1), ("w1", 2), ("w2", 0), ("w1", 3), ("w2", 1), ("p", 0), ("p", 1), ("w2", 2), ("w2", 3), ("g", 0), ("g", 1)):
+            load(what, i)
 
         x_grouped = keep.tile([P, T, PACK], BF16, align_bytes=64)
         x_codes = keep.tile([P, T], U32, align_bytes=64)
         x_scales = keep.tile([P, T], U8, align_bytes=64)
         for a in range(2):
-            for part, copy in ((0, nc.vector.tensor_copy), (1, nc.scalar.copy)):
-                c0 = part * 128
-                dst = x_grouped[:, a * HALF + c0 : a * HALF + c0 + 128, :]
-                src = x_raw[a][:, :, c0 : c0 + 128]
+            for copy, c0, c1 in ((nc.vector.tensor_copy, 0, X_VECTOR[a]), (nc.scalar.copy, X_VECTOR[a], HALF)):
+                dst = x_grouped[:, a * HALF + c0 : a * HALF + c1, :]
+                src = x_raw[a][:, :, c0:c1]
                 copy(out=dst.rearrange("p (c i) j -> p c j i", i=4), in_=src.rearrange("p j (c i) -> p c j i", i=4))
         for a in range(2):
             cols = slice(a * HALF, (a + 1) * HALF)
@@ -98,77 +96,82 @@ def tile_routed_moe_kernel(tc, xT, w1, w2, gate, offs, pos1, pos2, out):
             y_block = keep.tile([P, E * C], F32, name=f"y_slots{b}")
             y_slots.append(y_block)
 
-        w1_q = []
-        w2_q = []
-        g_q = []
+        w1_q = {}
+        w2_q = {}
+        h_grouped = {}
+        pieces = []
 
-        def interleave_w1(e):
-            grouped = four.tile([P, H * PACK], BF16, name="w1_grouped", align_bytes=64)
-            dst = grouped[:].rearrange("p (t m j) -> p m j t", t=PACK, j=PACK)
-            src = w1_raw[e][:].rearrange("p j (m t) -> p m j t", t=PACK)
-            nc.vector.tensor_copy(out=dst[:, :W1_VECTOR[e]], in_=src[:, :W1_VECTOR[e]])
-            nc.scalar.copy(out=dst[:, W1_VECTOR[e]:], in_=src[:, W1_VECTOR[e]:])
-            return grouped
-
-        def quantize_w1(grouped):
-            codes = four.tile([P, H], U32, name="w1_codes", align_bytes=64)
-            scales = four.tile([P, H], U8, name="w1_scales", align_bytes=64)
-            nc.vector.quantize_mx(out=codes[:].bitcast(FP8X4), scales=scales[:], in_=grouped[:])
-            w1_q.append((codes, scales))
-
-        def gather(e):
-            index = offs_sb[:, e * C // 16 : (e + 1) * C // 16]
-            codes = four.tile([P, C], U32, name="slot_codes", align_bytes=64)
-            scales = four.tile([P, C], U8, name="slot_scales", align_bytes=64)
+        def gather(k):
+            s0 = sum(PIECES[:k])
+            index = offs_sb[:, s0 // 16 : (s0 + PIECES[k]) // 16]
+            codes = keep.tile([P, PIECES[k]], U32, name=f"slot_codes{k}", align_bytes=64)
+            scales = keep.tile([P, PIECES[k]], U8, name=f"slot_scales{k}", align_bytes=64)
             nc.vector.tensor_copy(out=codes[:], in_=x_codes[:].indirect(index))
             nc.vector.tensor_copy(out=scales[:], in_=x_scales[:].indirect(index))
-            g_q.append((codes, scales))
+            pieces.append((s0, codes, scales))
 
-        def interleave_w2(e):
-            grouped = four.tile([P, N, PACK], BF16, name="w2_grouped", align_bytes=64)
-            copy = nc.vector.tensor_copy if W2_VECTOR[e] else nc.scalar.copy
-            copy(
+        def slots(s):
+            for s0, codes, scales in pieces:
+                if s0 <= s < s0 + codes.shape[1]:
+                    return codes[:, s - s0 : s - s0 + SLOTS], scales[:, s - s0 : s - s0 + SLOTS]
+
+        def quantize_w1(e):
+            grouped = keep.tile([P, H * PACK], BF16, name=f"w1_grouped{e}", align_bytes=64)
+            dst = grouped[:].rearrange("p (t m j) -> p m j t", t=PACK, j=PACK)
+            src = w1_raw[e][:].rearrange("p j (m t) -> p m j t", t=PACK)
+            v, g = W1_VECTOR[e], W1_GPSIMD[e]
+            for copy, m0, m1 in ((nc.vector.tensor_copy, 0, v), (gp_copy, v, v + g), (nc.scalar.copy, v + g, P)):
+                if m0 < m1:
+                    copy(out=dst[:, m0:m1], in_=src[:, m0:m1])
+            codes = keep.tile([P, H], U32, name=f"w1_codes{e}", align_bytes=64)
+            scales = keep.tile([P, H], U8, name=f"w1_scales{e}", align_bytes=64)
+            nc.vector.quantize_mx(out=codes[:].bitcast(FP8X4), scales=scales[:], in_=grouped[:])
+            w1_q[e] = (codes, scales)
+
+        def quantize_w2(e):
+            grouped = keep.tile([P, N, PACK], BF16, name=f"w2_grouped{e}", align_bytes=64)
+            copy_on[W2_ENGINE[e]](
                 out=grouped[:].rearrange("p (c i) j -> p c j i", i=4),
                 in_=w2_raw[e][:].rearrange("p j (c i) -> p c j i", i=4),
             )
-            return grouped
-
-        def quantize_w2(grouped):
-            codes = four.tile([P, N], U32, name="w2_codes", align_bytes=64)
-            scales = four.tile([P, N], U8, name="w2_scales", align_bytes=64)
+            codes = keep.tile([P, N], U32, name=f"w2_codes{e}", align_bytes=64)
+            scales = keep.tile([P, N], U8, name=f"w2_scales{e}", align_bytes=64)
             nc.vector.quantize_mx(
                 out=codes[:].bitcast(FP8X4), scales=scales[:], in_=grouped[:].rearrange("p n j -> p (n j)")
             )
-            w2_q.append((codes, scales))
+            w2_q[e] = (codes, scales)
 
         def first_layer(e):
-            grouped = four.tile([P, C, PACK], BF16, name="h_grouped", align_bytes=64)
-            for s in range(C // SLOTS):
-                cols = slice(s * SLOTS, (s + 1) * SLOTS)
+            h_grouped[e] = keep.tile([P, C, PACK], BF16, name=f"h_grouped{e}", align_bytes=64)
+            for s in range(0, C, SLOTS):
+                codes, scales = slots(e * C + s)
                 acc = psum.tile([P, PACK, SLOTS], F32, name="h_acc")
                 for t in range(PACK):
                     nc.tensor.matmul_mx(
                         out=acc[:, t, :],
                         lhsT=w1_q[e][0][:, t * P : (t + 1) * P].bitcast(FP8X4),
                         lhsT_scale=w1_q[e][1][:, t * P : (t + 1) * P],
-                        rhs=g_q[e][0][:, cols].bitcast(FP8X4),
-                        rhs_scale=g_q[e][1][:, cols],
+                        rhs=codes.bitcast(FP8X4),
+                        rhs_scale=scales,
                         start=True,
                         stop=True,
                     )
-                nc.scalar.activation(grouped[:, cols, :], acc[:].rearrange("p t n -> p n t"), SILU)
-            return grouped
+                nc.scalar.activation(h_grouped[e][:, s : s + SLOTS, :], acc[:].rearrange("p t n -> p n t"), SILU)
 
-        def second_layer(e, grouped):
-            codes = four.tile([P, C], U32, name="h_codes", align_bytes=64)
-            scales = four.tile([P, C], U8, name="h_scales", align_bytes=64)
+        y_acc = {}
+
+        def second_layer(e):
+            codes = keep.tile([P, C], U32, name=f"h_codes{e}", align_bytes=64)
+            scales = keep.tile([P, C], U8, name=f"h_scales{e}", align_bytes=64)
             nc.vector.quantize_mx(
-                out=codes[:].bitcast(FP8X4), scales=scales[:], in_=grouped[:].rearrange("p n t -> p (n t)")
+                out=codes[:].bitcast(FP8X4), scales=scales[:], in_=h_grouped[e][:].rearrange("p n t -> p (n t)")
             )
-            acc = psum.tile([P, BLOCKS, C], F32, name="y_acc")
+            pair = e // 2
             for b in range(BLOCKS):
+                if e % 2 == 0:
+                    y_acc[pair, b] = ysum.tile([P, 2, C], F32, name=f"y_acc{pair}{b}")
                 nc.tensor.matmul_mx(
-                    out=acc[:, b, :],
+                    out=y_acc[pair, b][:, e % 2, :],
                     lhsT=w2_q[e][0][:, b * P : (b + 1) * P].bitcast(FP8X4),
                     lhsT_scale=w2_q[e][1][:, b * P : (b + 1) * P],
                     rhs=codes[:].bitcast(FP8X4),
@@ -176,31 +179,29 @@ def tile_routed_moe_kernel(tc, xT, w1, w2, gate, offs, pos1, pos2, out):
                     start=True,
                     stop=True,
                 )
-            for b in range(BLOCKS):
-                nc.scalar.copy(out=y_slots[b][:, e * C : (e + 1) * C], in_=acc[:, b, :])
+                if e % 2 == 1:
+                    copy_on["SSVS"[2 * pair + b]](
+                        out=y_slots[b][:, 2 * pair * C : 2 * (pair + 1) * C],
+                        in_=y_acc[pair, b][:].rearrange("p e n -> p (e n)"),
+                    )
 
-        h_groups = []
         for e in range(E + 1):
             if e < E:
-                gather(e)
-                w1_grouped = interleave_w1(e)
-                quantize_w1(w1_grouped)
-                h_groups.append(first_layer(e))
+                if e < len(PIECES):
+                    gather(e)
+                quantize_w1(e)
+                first_layer(e)
             if e > 0:
-                w2_grouped = interleave_w2(e - 1)
-                quantize_w2(w2_grouped)
-                second_layer(e - 1, h_groups[e - 1])
+                quantize_w2(e - 1)
+                second_layer(e - 1)
 
         out_view = out.rearrange("(b p) t -> b p t", p=P)
-        parts = []
+        parts = {}
         for b in range(BLOCKS):
-            pair = []
             for r, index in ((0, pos1_sb), (1, pos2_sb)):
-                part = keep.tile([P, T], F32, name=f"part{b}{r}")
-                nc.vector.tensor_tensor(part[:], y_slots[b][:].indirect(index[:]), gates[b][:, r, :], MULT)
-                pair.append(part)
-            parts.append(pair)
+                parts[b, r] = keep.tile([P, T], F32, name=f"part{b}{r}")
+                nc.vector.tensor_tensor(parts[b, r][:], y_slots[b][:].indirect(index[:]), gates[b][:, r, :], MULT)
         for b in range(BLOCKS):
             total = keep.tile([P, T], F32, name=f"total{b}")
-            nc.vector.tensor_add(out=total[:], in0=parts[b][0][:], in1=parts[b][1][:])
+            nc.vector.tensor_add(out=total[:], in0=parts[b, 0][:], in1=parts[b, 1][:])
             nc.sync.dma_start(out=out_view[b], in_=total[:])

@@ -1,6 +1,7 @@
 from contextlib import ExitStack
 
 import concourse.mybir as mybir
+from concourse.masks import make_identity
 
 K, T, E, C, H, N = 512, 512, 4, 256, 512, 256
 FLOPS = 2 * E * C * (K * H + H * N)
@@ -10,10 +11,13 @@ PACK = 4
 HALF = T // 2
 SLOTS = 128
 BLOCKS = N // P
-X_VECTOR = (192, 128)
-W1_VECTOR = (0, 16, 56, 128)
+X_VECTOR = (192, 192)
+W1_VECTOR = (0, 0, 128, 56)
 W1_GPSIMD = (0, 0, 0, 0)
-W2_ENGINE = "VSVV"
+W2_VECTOR = (192, 64, 256, 256)
+W2_GPSIMD = (0, 0, 0, 0)
+SUM_TENSOR = 384
+EVAC = "SSSSVS"
 PIECES = (384, 384, 256)
 
 F32 = mybir.dt.float32
@@ -32,7 +36,7 @@ def tile_routed_moe_kernel(tc, xT, w1, w2, gate, offs, pos1, pos2, out):
     with ExitStack() as ctx:
         lists = ctx.enter_context(tc.tile_pool(name="lists", bufs=1))
         keep = ctx.enter_context(tc.tile_pool(name="keep", bufs=1))
-        psum = ctx.enter_context(tc.psum_pool(name="psum", bufs=4))
+        psum = ctx.enter_context(tc.psum_pool(name="psum", bufs=3))
         ysum = ctx.enter_context(tc.psum_pool(name="ysum", bufs=1))
 
         offs_sb = lists.tile([P, E * C // 16], U16)
@@ -42,6 +46,9 @@ def tile_routed_moe_kernel(tc, xT, w1, w2, gate, offs, pos1, pos2, out):
         dummy = keep.tile([P, 2], F32)
         nc.gpsimd.memset(dummy[:], 0.0)
         nc.scalar.activation(dummy[:, 1:2], dummy[:, 0:1], SILU)
+
+        ident = keep.tile([P, P], F32)
+        make_identity(nc, ident[:])
 
         def gp_copy(out, in_):
             nc.gpsimd.tensor_scalar(out=out, in0=in_, scalar1=1.0, scalar2=0.0, op0=MULT, op1=ADD)
@@ -72,7 +79,7 @@ def tile_routed_moe_kernel(tc, xT, w1, w2, gate, offs, pos1, pos2, out):
             elif what == "p":
                 nc.sync.dma_start(out=(pos1_sb if i == 0 else pos2_sb)[:], in_=(pos1 if i == 0 else pos2))
 
-        for what, i in (("x", 0), ("o", 0), ("x", 1), ("w1", 0), ("w1", 1), ("w1", 2), ("w2", 0), ("w1", 3), ("w2", 1), ("p", 0), ("p", 1), ("w2", 2), ("w2", 3), ("g", 0), ("g", 1)):
+        for what, i in (("x", 0), ("x", 1), ("o", 0), ("w1", 0), ("w1", 1), ("w2", 0), ("w1", 2), ("w1", 3), ("w2", 1), ("p", 0), ("w2", 2), ("w2", 3), ("p", 1), ("g", 0), ("g", 1)):
             load(what, i)
 
         x_grouped = keep.tile([P, T, PACK], BF16, align_bytes=64)
@@ -130,10 +137,13 @@ def tile_routed_moe_kernel(tc, xT, w1, w2, gate, offs, pos1, pos2, out):
 
         def quantize_w2(e):
             grouped = keep.tile([P, N, PACK], BF16, name=f"w2_grouped{e}", align_bytes=64)
-            copy_on[W2_ENGINE[e]](
-                out=grouped[:].rearrange("p (c i) j -> p c j i", i=4),
-                in_=w2_raw[e][:].rearrange("p j (c i) -> p c j i", i=4),
-            )
+            v, g = W2_VECTOR[e], W2_GPSIMD[e]
+            for copy, c0, c1 in ((nc.vector.tensor_copy, 0, v), (gp_copy, v, v + g), (nc.scalar.copy, v + g, N)):
+                if c0 < c1:
+                    copy(
+                        out=grouped[:, c0:c1, :].rearrange("p (c i) j -> p c j i", i=4),
+                        in_=w2_raw[e][:, :, c0:c1].rearrange("p j (c i) -> p c j i", i=4),
+                    )
             codes = keep.tile([P, N], U32, name=f"w2_codes{e}", align_bytes=64)
             scales = keep.tile([P, N], U8, name=f"w2_scales{e}", align_bytes=64)
             nc.vector.quantize_mx(
@@ -166,12 +176,20 @@ def tile_routed_moe_kernel(tc, xT, w1, w2, gate, offs, pos1, pos2, out):
             nc.vector.quantize_mx(
                 out=codes[:].bitcast(FP8X4), scales=scales[:], in_=h_grouped[e][:].rearrange("p n t -> p (n t)")
             )
-            pair = e // 2
             for b in range(BLOCKS):
-                if e % 2 == 0:
-                    y_acc[pair, b] = ysum.tile([P, 2, C], F32, name=f"y_acc{pair}{b}")
+                if e < 2:
+                    if e == 0:
+                        y_acc[b] = ysum.tile([P, 2, C], F32, name=f"y_acc{b}")
+                    acc = y_acc[b][:, e, :]
+                elif e == 2:
+                    if b == 0:
+                        y_acc[2] = ysum.tile([P, 2, C], F32, name="y_acc2")
+                    acc = y_acc[2][:, b, :]
+                else:
+                    y_acc[3 + b] = ysum.tile([P, C], F32, name=f"y_acc{3 + b}")
+                    acc = y_acc[3 + b][:]
                 nc.tensor.matmul_mx(
-                    out=y_acc[pair, b][:, e % 2, :],
+                    out=acc,
                     lhsT=w2_q[e][0][:, b * P : (b + 1) * P].bitcast(FP8X4),
                     lhsT_scale=w2_q[e][1][:, b * P : (b + 1) * P],
                     rhs=codes[:].bitcast(FP8X4),
@@ -179,11 +197,14 @@ def tile_routed_moe_kernel(tc, xT, w1, w2, gate, offs, pos1, pos2, out):
                     start=True,
                     stop=True,
                 )
-                if e % 2 == 1:
-                    copy_on["SSVS"[2 * pair + b]](
-                        out=y_slots[b][:, 2 * pair * C : 2 * (pair + 1) * C],
-                        in_=y_acc[pair, b][:].rearrange("p e n -> p (e n)"),
-                    )
+            cols = slice(e * C, (e + 1) * C)
+            for b in range(BLOCKS):
+                if e == 1:
+                    copy_on[EVAC[b]](out=y_slots[b][:, : 2 * C], in_=y_acc[b][:].rearrange("p e n -> p (e n)"))
+                elif e == 2:
+                    copy_on[EVAC[2 + b]](out=y_slots[b][:, cols], in_=y_acc[2][:, b, :])
+                elif e == 3:
+                    copy_on[EVAC[4 + b]](out=y_slots[b][:, cols], in_=y_acc[3 + b][:])
 
         for e in range(E + 1):
             if e < E:
@@ -196,12 +217,34 @@ def tile_routed_moe_kernel(tc, xT, w1, w2, gate, offs, pos1, pos2, out):
                 second_layer(e - 1)
 
         out_view = out.rearrange("(b p) t -> b p t", p=P)
-        parts = {}
-        for b in range(BLOCKS):
-            for r, index in ((0, pos1_sb), (1, pos2_sb)):
-                parts[b, r] = keep.tile([P, T], F32, name=f"part{b}{r}")
-                nc.vector.tensor_tensor(parts[b, r][:], y_slots[b][:].indirect(index[:]), gates[b][:, r, :], MULT)
-        for b in range(BLOCKS):
-            total = keep.tile([P, T], F32, name=f"total{b}")
-            nc.vector.tensor_add(out=total[:], in0=parts[b, 0][:], in1=parts[b, 1][:])
-            nc.sync.dma_start(out=out_view[b], in_=total[:])
+
+        def fetch(b, r, t0, t1):
+            index = (pos1_sb, pos2_sb)[r]
+            part = keep.tile([P, t1 - t0], F32, name=f"part{b}{r}{t0}")
+            nc.vector.tensor_tensor(
+                part[:], y_slots[b][:].indirect(index[:, t0 // 16 : t1 // 16]), gates[b][:, r, t0:t1], MULT
+            )
+            return part
+
+        first0 = fetch(0, 0, 0, T)
+        second0 = fetch(0, 1, 0, T)
+        sum0 = ysum.tile([P, SUM_TENSOR], F32, name="y_acc0")
+        nc.tensor.matmul(sum0[:], ident[:], first0[:, :SUM_TENSOR], start=True, stop=False)
+        nc.tensor.matmul(sum0[:], ident[:], second0[:, :SUM_TENSOR], start=False, stop=True)
+        total00 = keep.tile([P, SUM_TENSOR], F32, name="total00")
+        nc.scalar.copy(out=total00[:], in_=sum0[:])
+        nc.sync.dma_start(out=out_view[0][:, :SUM_TENSOR], in_=total00[:])
+        total01 = keep.tile([P, T - SUM_TENSOR], F32, name="total01")
+        nc.vector.tensor_add(out=total01[:], in0=first0[:, SUM_TENSOR:], in1=second0[:, SUM_TENSOR:])
+        nc.sync.dma_start(out=out_view[0][:, SUM_TENSOR:], in_=total01[:])
+
+        first1 = fetch(1, 0, 0, T)
+        seconds = []
+        for t0 in range(0, T, HALF):
+            second1 = fetch(1, 1, t0, t0 + HALF)
+            seconds.append(second1)
+        for a in range(2):
+            cols = slice(a * HALF, (a + 1) * HALF)
+            total1 = keep.tile([P, HALF], F32, name=f"total1{a}")
+            nc.vector.tensor_add(out=total1[:], in0=first1[:, cols], in1=seconds[a][:])
+            nc.sync.dma_start(out=out_view[1][:, cols], in_=total1[:])

@@ -17,6 +17,7 @@ W1_GPSIMD = (0, 0, 0, 0)
 W2_VECTOR = (192, 64, 256, 256)
 W2_GPSIMD = (0, 0, 0, 0)
 SUM_TENSOR = 384
+SPLIT = 192
 EVAC = "SSSSVS"
 PIECES = (384, 384, 256)
 
@@ -79,7 +80,7 @@ def tile_routed_moe_kernel(tc, xT, w1, w2, gate, offs, pos1, pos2, out):
             elif what == "p":
                 nc.sync.dma_start(out=(pos1_sb if i == 0 else pos2_sb)[:], in_=(pos1 if i == 0 else pos2))
 
-        for what, i in (("x", 0), ("x", 1), ("o", 0), ("w1", 0), ("w1", 1), ("w2", 0), ("w1", 2), ("w1", 3), ("w2", 1), ("p", 0), ("w2", 2), ("w2", 3), ("p", 1), ("g", 0), ("g", 1)):
+        for what, i in (("x", 0), ("x", 1), ("o", 0), ("w1", 0), ("w1", 1), ("w2", 0), ("w1", 2), ("w1", 3), ("w2", 1), ("w2", 2), ("w2", 3), ("g", 0), ("p", 0), ("p", 1), ("g", 1)):
             load(what, i)
 
         x_grouped = keep.tile([P, T, PACK], BF16, align_bytes=64)
@@ -239,12 +240,14 @@ def tile_routed_moe_kernel(tc, xT, w1, w2, gate, offs, pos1, pos2, out):
         nc.sync.dma_start(out=out_view[0][:, SUM_TENSOR:], in_=total01[:])
 
         first1 = fetch(1, 0, 0, T)
-        seconds = []
-        for t0 in range(0, T, HALF):
-            second1 = fetch(1, 1, t0, t0 + HALF)
-            seconds.append(second1)
-        for a in range(2):
-            cols = slice(a * HALF, (a + 1) * HALF)
-            total1 = keep.tile([P, HALF], F32, name=f"total1{a}")
-            nc.vector.tensor_add(out=total1[:], in0=first1[:, cols], in1=seconds[a][:])
-            nc.sync.dma_start(out=out_view[1][:, cols], in_=total1[:])
+        second10 = fetch(1, 1, 0, SPLIT)
+        sum1 = ysum.tile([P, SPLIT], F32, name="y_acc1")
+        nc.tensor.matmul(sum1[:], ident[:], first1[:, :SPLIT], start=True, stop=False)
+        nc.tensor.matmul(sum1[:], ident[:], second10[:], start=False, stop=True)
+        total10 = keep.tile([P, SPLIT], F32, name="total10")
+        nc.scalar.copy(out=total10[:], in_=sum1[:])
+        nc.sync.dma_start(out=out_view[1][:, :SPLIT], in_=total10[:])
+        second11 = fetch(1, 1, SPLIT, T)
+        total11 = keep.tile([P, T - SPLIT], F32, name="total11")
+        nc.vector.tensor_add(out=total11[:], in0=first1[:, SPLIT:], in1=second11[:])
+        nc.sync.dma_start(out=out_view[1][:, SPLIT:], in_=total11[:])

from contextlib import ExitStack

import concourse.mybir as mybir
from concourse.masks import make_identity

K, T, E, C, H, N = 512, 512, 4, 256, 512, 256
FLOPS = 2 * E * C * (K * H + H * N)

P = 128
PACK = 4
HALF = T // 2
SLOTS = 128
BLOCKS = N // P
X_VECTOR = (192, 192)
W1_VECTOR = (0, 0, 128, 56)
W1_GPSIMD = (0, 0, 0, 0)
W2_VECTOR = (192, 64, 256, 256)
W2_GPSIMD = (0, 0, 0, 0)
SUM_TENSOR = 384
SPLIT = 192
EVAC = "SSSSVS"
PIECES = (384, 384, 256)

F32 = mybir.dt.float32
BF16 = mybir.dt.bfloat16
U32 = mybir.dt.uint32
U16 = mybir.dt.uint16
U8 = mybir.dt.uint8
FP8X4 = mybir.dt.float8_e4m3fn_x4
MULT = mybir.AluOpType.mult
ADD = mybir.AluOpType.add
SILU = mybir.ActivationFunctionType.Silu


def tile_routed_moe_kernel(tc, xT, w1, w2, gate, offs, pos1, pos2, out):
    nc = tc.nc
    with ExitStack() as ctx:
        lists = ctx.enter_context(tc.tile_pool(name="lists", bufs=1))
        keep = ctx.enter_context(tc.tile_pool(name="keep", bufs=1))
        psum = ctx.enter_context(tc.psum_pool(name="psum", bufs=3))
        ysum = ctx.enter_context(tc.psum_pool(name="ysum", bufs=1))

        offs_sb = lists.tile([P, E * C // 16], U16)
        pos1_sb = lists.tile([P, T // 16], U16)
        pos2_sb = lists.tile([P, T // 16], U16)

        dummy = keep.tile([P, 2], F32)
        nc.gpsimd.memset(dummy[:], 0.0)
        nc.scalar.activation(dummy[:, 1:2], dummy[:, 0:1], SILU)

        ident = keep.tile([P, P], F32)
        make_identity(nc, ident[:])

        def gp_copy(out, in_):
            nc.gpsimd.tensor_scalar(out=out, in0=in_, scalar1=1.0, scalar2=0.0, op0=MULT, op1=ADD)

        copy_on = {"V": nc.vector.tensor_copy, "S": nc.scalar.copy, "G": gp_copy}

        x_view = xT.rearrange("(p j) t -> p j t", j=PACK)
        x_raw = {}
        w1_raw = {}
        w2_raw = {}
        gates = {}

        def load(what, i):
            if what == "x":
                x_raw[i] = keep.tile([P, PACK, HALF], F32, name=f"x_raw{i}")
                nc.sync.dma_start(out=x_raw[i][:], in_=x_view[:, :, i * HALF : (i + 1) * HALF])
            elif what == "w1":
                w1_raw[i] = keep.tile([P, PACK, H], F32, name=f"w1_raw{i}")
                nc.sync.dma_start(out=w1_raw[i][:], in_=w1[i].rearrange("(p j) h -> p j h", j=PACK))
            elif what == "w2":
                w2_raw[i] = keep.tile([P, PACK, N], F32, name=f"w2_raw{i}")
                nc.sync.dma_start(out=w2_raw[i][:], in_=w2[i].rearrange("(p j) n -> p j n", j=PACK))
            elif what == "g":
                gates[i] = keep.tile([P, 2, T], F32, name=f"gate{i}")
                nc.sync.dma_start(out=gates[i][:], in_=gate[:, i * P : (i + 1) * P, :].rearrange("g p t -> p g t"))
            elif what == "o":
                nc.sync.dma_start(out=offs_sb[:], in_=offs)
            elif what == "p":
                nc.sync.dma_start(out=(pos1_sb if i == 0 else pos2_sb)[:], in_=(pos1 if i == 0 else pos2))

        for what, i in (("x", 0), ("x", 1), ("o", 0), ("w1", 0), ("w1", 1), ("w2", 0), ("w1", 2), ("w1", 3), ("w2", 1), ("w2", 2), ("w2", 3), ("g", 0), ("p", 0), ("p", 1), ("g", 1)):
            load(what, i)

        x_grouped = keep.tile([P, T, PACK], BF16, align_bytes=64)
        x_codes = keep.tile([P, T], U32, align_bytes=64)
        x_scales = keep.tile([P, T], U8, align_bytes=64)
        for a in range(2):
            for copy, c0, c1 in ((nc.vector.tensor_copy, 0, X_VECTOR[a]), (nc.scalar.copy, X_VECTOR[a], HALF)):
                dst = x_grouped[:, a * HALF + c0 : a * HALF + c1, :]
                src = x_raw[a][:, :, c0:c1]
                copy(out=dst.rearrange("p (c i) j -> p c j i", i=4), in_=src.rearrange("p j (c i) -> p c j i", i=4))
        for a in range(2):
            cols = slice(a * HALF, (a + 1) * HALF)
            nc.vector.quantize_mx(
                out=x_codes[:, cols].bitcast(FP8X4),
                scales=x_scales[:, cols],
                in_=x_grouped[:, cols, :].rearrange("p t j -> p (t j)"),
            )

        y_slots = []
        for b in range(BLOCKS):
            y_block = keep.tile([P, E * C], F32, name=f"y_slots{b}")
            y_slots.append(y_block)

        w1_q = {}
        w2_q = {}
        h_grouped = {}
        pieces = []

        def gather(k):
            s0 = sum(PIECES[:k])
            index = offs_sb[:, s0 // 16 : (s0 + PIECES[k]) // 16]
            codes = keep.tile([P, PIECES[k]], U32, name=f"slot_codes{k}", align_bytes=64)
            scales = keep.tile([P, PIECES[k]], U8, name=f"slot_scales{k}", align_bytes=64)
            nc.vector.tensor_copy(out=codes[:], in_=x_codes[:].indirect(index))
            nc.vector.tensor_copy(out=scales[:], in_=x_scales[:].indirect(index))
            pieces.append((s0, codes, scales))

        def slots(s):
            for s0, codes, scales in pieces:
                if s0 <= s < s0 + codes.shape[1]:
                    return codes[:, s - s0 : s - s0 + SLOTS], scales[:, s - s0 : s - s0 + SLOTS]

        def quantize_w1(e):
            grouped = keep.tile([P, H * PACK], BF16, name=f"w1_grouped{e}", align_bytes=64)
            dst = grouped[:].rearrange("p (t m j) -> p m j t", t=PACK, j=PACK)
            src = w1_raw[e][:].rearrange("p j (m t) -> p m j t", t=PACK)
            v, g = W1_VECTOR[e], W1_GPSIMD[e]
            for copy, m0, m1 in ((nc.vector.tensor_copy, 0, v), (gp_copy, v, v + g), (nc.scalar.copy, v + g, P)):
                if m0 < m1:
                    copy(out=dst[:, m0:m1], in_=src[:, m0:m1])
            codes = keep.tile([P, H], U32, name=f"w1_codes{e}", align_bytes=64)
            scales = keep.tile([P, H], U8, name=f"w1_scales{e}", align_bytes=64)
            nc.vector.quantize_mx(out=codes[:].bitcast(FP8X4), scales=scales[:], in_=grouped[:])
            w1_q[e] = (codes, scales)

        def quantize_w2(e):
            grouped = keep.tile([P, N, PACK], BF16, name=f"w2_grouped{e}", align_bytes=64)
            v, g = W2_VECTOR[e], W2_GPSIMD[e]
            for copy, c0, c1 in ((nc.vector.tensor_copy, 0, v), (gp_copy, v, v + g), (nc.scalar.copy, v + g, N)):
                if c0 < c1:
                    copy(
                        out=grouped[:, c0:c1, :].rearrange("p (c i) j -> p c j i", i=4),
                        in_=w2_raw[e][:, :, c0:c1].rearrange("p j (c i) -> p c j i", i=4),
                    )
            codes = keep.tile([P, N], U32, name=f"w2_codes{e}", align_bytes=64)
            scales = keep.tile([P, N], U8, name=f"w2_scales{e}", align_bytes=64)
            nc.vector.quantize_mx(
                out=codes[:].bitcast(FP8X4), scales=scales[:], in_=grouped[:].rearrange("p n j -> p (n j)")
            )
            w2_q[e] = (codes, scales)

        def first_layer(e):
            h_grouped[e] = keep.tile([P, C, PACK], BF16, name=f"h_grouped{e}", align_bytes=64)
            for s in range(0, C, SLOTS):
                codes, scales = slots(e * C + s)
                acc = psum.tile([P, PACK, SLOTS], F32, name="h_acc")
                for t in range(PACK):
                    nc.tensor.matmul_mx(
                        out=acc[:, t, :],
                        lhsT=w1_q[e][0][:, t * P : (t + 1) * P].bitcast(FP8X4),
                        lhsT_scale=w1_q[e][1][:, t * P : (t + 1) * P],
                        rhs=codes.bitcast(FP8X4),
                        rhs_scale=scales,
                        start=True,
                        stop=True,
                    )
                nc.scalar.activation(h_grouped[e][:, s : s + SLOTS, :], acc[:].rearrange("p t n -> p n t"), SILU)

        y_acc = {}

        def second_layer(e):
            codes = keep.tile([P, C], U32, name=f"h_codes{e}", align_bytes=64)
            scales = keep.tile([P, C], U8, name=f"h_scales{e}", align_bytes=64)
            nc.vector.quantize_mx(
                out=codes[:].bitcast(FP8X4), scales=scales[:], in_=h_grouped[e][:].rearrange("p n t -> p (n t)")
            )
            for b in range(BLOCKS):
                if e < 2:
                    if e == 0:
                        y_acc[b] = ysum.tile([P, 2, C], F32, name=f"y_acc{b}")
                    acc = y_acc[b][:, e, :]
                elif e == 2:
                    if b == 0:
                        y_acc[2] = ysum.tile([P, 2, C], F32, name="y_acc2")
                    acc = y_acc[2][:, b, :]
                else:
                    y_acc[3 + b] = ysum.tile([P, C], F32, name=f"y_acc{3 + b}")
                    acc = y_acc[3 + b][:]
                nc.tensor.matmul_mx(
                    out=acc,
                    lhsT=w2_q[e][0][:, b * P : (b + 1) * P].bitcast(FP8X4),
                    lhsT_scale=w2_q[e][1][:, b * P : (b + 1) * P],
                    rhs=codes[:].bitcast(FP8X4),
                    rhs_scale=scales[:],
                    start=True,
                    stop=True,
                )
            cols = slice(e * C, (e + 1) * C)
            for b in range(BLOCKS):
                if e == 1:
                    copy_on[EVAC[b]](out=y_slots[b][:, : 2 * C], in_=y_acc[b][:].rearrange("p e n -> p (e n)"))
                elif e == 2:
                    copy_on[EVAC[2 + b]](out=y_slots[b][:, cols], in_=y_acc[2][:, b, :])
                elif e == 3:
                    copy_on[EVAC[4 + b]](out=y_slots[b][:, cols], in_=y_acc[3 + b][:])

        for e in range(E + 1):
            if e < E:
                if e < len(PIECES):
                    gather(e)
                quantize_w1(e)
                first_layer(e)
            if e > 0:
                quantize_w2(e - 1)
                second_layer(e - 1)

        out_view = out.rearrange("(b p) t -> b p t", p=P)

        def fetch(b, r, t0, t1):
            index = (pos1_sb, pos2_sb)[r]
            part = keep.tile([P, t1 - t0], F32, name=f"part{b}{r}{t0}")
            nc.vector.tensor_tensor(
                part[:], y_slots[b][:].indirect(index[:, t0 // 16 : t1 // 16]), gates[b][:, r, t0:t1], MULT
            )
            return part

        first0 = fetch(0, 0, 0, T)
        second0 = fetch(0, 1, 0, T)
        sum0 = ysum.tile([P, SUM_TENSOR], F32, name="y_acc0")
        nc.tensor.matmul(sum0[:], ident[:], first0[:, :SUM_TENSOR], start=True, stop=False)
        nc.tensor.matmul(sum0[:], ident[:], second0[:, :SUM_TENSOR], start=False, stop=True)
        total00 = keep.tile([P, SUM_TENSOR], F32, name="total00")
        nc.scalar.copy(out=total00[:], in_=sum0[:])
        nc.sync.dma_start(out=out_view[0][:, :SUM_TENSOR], in_=total00[:])
        total01 = keep.tile([P, T - SUM_TENSOR], F32, name="total01")
        nc.vector.tensor_add(out=total01[:], in0=first0[:, SUM_TENSOR:], in1=second0[:, SUM_TENSOR:])
        nc.sync.dma_start(out=out_view[0][:, SUM_TENSOR:], in_=total01[:])

        first1 = fetch(1, 0, 0, T)
        second10 = fetch(1, 1, 0, SPLIT)
        sum1 = ysum.tile([P, SPLIT], F32, name="y_acc1")
        nc.tensor.matmul(sum1[:], ident[:], first1[:, :SPLIT], start=True, stop=False)
        nc.tensor.matmul(sum1[:], ident[:], second10[:], start=False, stop=True)
        total10 = keep.tile([P, SPLIT], F32, name="total10")
        nc.scalar.copy(out=total10[:], in_=sum1[:])
        nc.sync.dma_start(out=out_view[1][:, :SPLIT], in_=total10[:])
        second11 = fetch(1, 1, SPLIT, T)
        total11 = keep.tile([P, T - SPLIT], F32, name="total11")
        nc.vector.tensor_add(out=total11[:], in0=first1[:, SPLIT:], in1=second11[:])
        nc.sync.dma_start(out=out_view[1][:, SPLIT:], in_=total11[:])
